import numpy as np
CORES = [34,162,290,418,42,426]
N = 6
TK = 128
NT = N * TK
EPS = 0.01
def setup_inputs(rng):
    x = (rng.standard_normal((N, 128, TK), dtype=np.float32) * (0.5 + np.arange(N, dtype=np.float32).reshape(N, 1, 1) / N) + rng.standard_normal((N, 128, 1), dtype=np.float32))
    return {"x": x}
def setup_inputs_big(rng):
    d = setup_inputs(rng)
    for k in ("x",): d[k] = (d[k].astype(np.float32) * 1024.0).astype(d[k].dtype)
    return d
def setup_inputs_small(rng):
    d = setup_inputs(rng)
    for k in ("x",): d[k] = (d[k].astype(np.float32) * (1 / 1024.0)).astype(d[k].dtype)
    return d
def setup_inputs_apart(rng):
    d = setup_inputs(rng)
    f = (10.0 ** rng.permutation(np.linspace(-1.5, 1.5, N))).astype(np.float32).reshape(N, 1, 1)
    for k in ("x",): d[k] = (d[k].astype(np.float32) * f).astype(d[k].dtype)
    return d
def setup_inputs_mixed(rng):
    d = setup_inputs(rng)
    f = (10.0 ** rng.uniform(-3, 3, (1, 128, 1))).astype(np.float32); shape = rng.integers(3, size=(1, 128, 1))
    for k in ("x",):
        x = d[k].astype(np.float32)
        m = x.mean(axis=(0, 2), keepdims=True); level = m + np.sign(x - m) * np.abs(x - m).mean(axis=(0, 2), keepdims=True) * rng.uniform(0.9, 1.1, x.shape).astype(np.float32)
        other = x * np.where(rng.random(x.shape) < 0.5, 0.1, 1.0).astype(np.float32)
        d[k] = (np.where(shape == 1, level, np.where(shape == 2, other, x)) * f).astype(d[k].dtype)
    return d
def setup_inputs_offset(rng):
    d = setup_inputs(rng)
    x = d["x"]; spread = x.std(axis=(0, 2), keepdims=True)
    d["x"] = (x + spread * rng.uniform(16, 48, (1, 128, 1)) * rng.choice([-1.0, 1.0], (1, 128, 1))).astype(np.float32)
    return d
def reference(x):
    X = x.astype(np.float64)
    mu = X.sum(axis=(0, 2)).reshape(1, 128, 1) / NT
    rs = 1.0 / np.sqrt(((X - mu) ** 2).sum(axis=(0, 2)).reshape(1, 128, 1) / NT + EPS)
    n = (X - mu) * rs
    return {"y": n.astype(np.float32)}

@@ -1,0 +1,197 @@
+import math
+from concourse.bass import DstId, RemoteDMATransfer
+from concourse.mybir import AluOpType, AxisListType, ActivationFunctionType
+
+N = 6
+TK = 128
+EPS = 0.01
+KT = 64
+ENGINES = 8
+
+SEED2, SEED1, SEED0 = 6707.0017479, -420.44720354, 10.68373326
+
+SCRATCH = {
+    "xs": ("sbuf", [128, TK], "float32"),
+    "xc": ("sbuf", [128, TK], "float32"),
+    "ys": ("sbuf", [128, TK], "float32"),
+    "st": ("sbuf", [128, 16], "float32"),
+    "two": ("sbuf", [128, KT], "float32"),
+    "tab": ("sbuf", [128, KT], "float32"),
+    "cmp": ("sbuf", [128, KT], "float32"),
+    "sm": ("sbuf", [128, 32], "float32"),
+}
+SEMAPHORES = ["ld", "a1", "a2", "p1", "p2", "snt", "vt", "vs", "at0", "aq", "anm", "axc", "as2", "az", "vq", "vy", "ay",
+              "stq"]
+
+
+def _links(topo, a, b):
+    if topo.mates(a, b) or topo.same_plane(a, b):
+        return 1
+    if topo.rack(topo.host(a)) == topo.rack(topo.host(b)):
+        return 2
+    return 1 if topo.chip(a) == topo.chip(b) else 3
+
+
+def _matchings(items):
+    if not items:
+        return [[]]
+    a, out = items[0], []
+    for b in items[1:]:
+        rest = [i for i in items[1:] if i != b]
+        out += [[(a, b)] + m for m in _matchings(rest)]
+    return out
+
+
+def _products(opts):
+    out = [[]]
+    for o in opts:
+        out = [p + [c] for p in out for c in o]
+    return out
+
+
+def _plan(cores, topo):
+    n = len(cores)
+
+    def ok(a, b):
+        return topo.may_write(cores[a], cores[b])
+
+    def ln(a, b):
+        return _links(topo, cores[a], cores[b])
+
+    best = None
+    for m in _matchings(list(range(n))):
+        if not all(ok(a, b) and ok(b, a) for a, b in m):
+            continue
+        needs = [(b, p) for b in range(n) for p in m if b not in p]
+        opts = [[c for c in p if ok(c, b)] for b, p in needs]
+        if not all(opts):
+            continue
+        hop1 = sum(ln(a, b) + ln(b, a) for a, b in m)
+        for pick in _products(opts):
+            cost = (max(pick.count(c) for c in range(n)), hop1, sum(ln(c, bp[0]) for c, bp in zip(pick, needs)))
+            if best is None or cost < best[0]:
+                best = (cost, m, [(c, bp[0]) for c, bp in zip(pick, needs)])
+    return best[1], best[2]
+
+
+def _engines(mask, most):
+    out, k, e = 0, 0, 0
+    while mask >> e:
+        if (mask >> e) & 1 and k < most:
+            out |= 1 << e
+            k += 1
+        e += 1
+    return out
+
+
+def _count(mask):
+    return bin(mask).count("1")
+
+
+def rank_program(g, core, T, topo):
+    rank = T.rank_of(core)
+    if rank is None:
+        return
+    cores = list(T.cores)
+    pairs, hop2 = _plan(cores, topo)
+    partner = [b if a == rank else a for a, b in pairs if rank in (a, b)][0]
+
+    def mask1(src, dst):
+        return _engines(topo.mask(cores[src], cores[dst]), ENGINES)
+
+    def mask2(src):
+        ms = [topo.mask(cores[src], cores[b]) for c, b in hop2 if c == src]
+        m = ms[0]
+        for o in ms[1:]:
+            m &= o
+        return _engines(m, ENGINES)
+
+    def slot(src, dst):
+        k = sorted(c for c, b in hop2 if b == dst).index(src)
+        return T.st[:, 6 + 4 * k:10 + 4 * k]
+
+    in1 = _count(mask1(partner, rank))
+    in2 = sum(_count(mask2(c)) for c, b in hop2 if b == rank)
+
+    S, V, A, Y = g.sync, g.vector, g.scalar, T.sem
+    F, OP = ActivationFunctionType, AluOpType
+    sm = T.sm
+    t0, sS, sQ, nmu, v, s, gg, pp, y0, t1, y1, t2, rs, s2, z1 = [sm[:, i:i + 1] for i in range(15)]
+    nms, m2s = T.st[:, 2:14:2], T.st[:, 3:14:2]
+    H = TK // 2
+
+    S.dma_start(T.xs[:], T.x[:]).then_inc(Y.ld, 16)
+
+    V.memset(T.two[:], 2.0).then_inc(Y.vt, 1)
+    V.wait_ge(Y.vt, 1)
+    V.tensor_tensor_scan(T.tab[:], T.two[:], T.two[:], 2.0 ** -7, OP.mult, OP.mult).then_inc(Y.vt, 1)
+    V.wait_ge(Y.vt, 2)
+
+    A.wait_ge(Y.ld, 16)
+    A.activation(T.xc[:], T.xs[:], F.Identity, scale=-1.0 / TK, accum_out=T.st[:, 2:3]).then_inc(Y.a1, 1)
+    A.wait_ge(Y.a1, 1)
+    A.activation(T.xc[:], T.xs[:], F.Square, bias=T.st[:, 2:3], accum_out=T.st[:, 3:4]).then_inc(Y.a2, 1)
+
+    g.wait_ge(Y.a2, 1)
+    rid, pid = topo.addr(cores[partner], core)
+    g.remote_dma(T.st[:, 4:6], T.st[:, 2:4], Y.p1, Y.snt, pid, rid, mask1(rank, partner))
+    g.wait_ge(Y.p1, in1)
+    outs = [b for c, b in hop2 if c == rank]
+    ids = []
+    for b in outs:
+        rid, pid = topo.addr(cores[b], core)
+        ids.append(DstId(rid=rid, pnc=pid))
+    g.remote_dma_fused([RemoteDMATransfer(dst_ids=ids, dma_engine_mask=mask2(rank), remote_sem=Y.p2,
+                                          srcs=[T.st[:, 2:6]], dsts=[slot(rank, b) for b in outs], alu_op=0)],
+                       local_sem=Y.snt)
+    g.wait_ge(Y.snt, _count(mask1(rank, partner)) + _count(mask2(rank)))
+
+    A.wait_ge(Y.a2, 1)
+    A.wait_ge(Y.p1, in1)
+    A.wait_ge(Y.p2, in2)
+    A.activation(sm[:, 16:22], m2s, F.Identity, bias=EPS / N, scale=1.0 / (N * TK), accum_out=t0).then_inc(Y.at0, 1)
+    A.wait_ge(Y.vs, 1)
+    A.activation(sm[:, 24:30], nms, F.Square, bias=sS, scale=-float(N), accum_out=sQ).then_inc(Y.aq, 1)
+    A.activation(nmu, sS, F.Identity, scale=1.0 / N).then_inc(Y.anm, 1)
+    A.wait_ge(Y.anm, 1)
+    A.activation(T.xc[:], T.xs[:], F.Identity, bias=nmu).then_inc(Y.axc, 1)
+    A.wait_ge(Y.vq, 3)
+    A.activation(s2, s, F.Identity, scale=math.sqrt(2.0)).then_inc(Y.as2, 1)
+    A.wait_ge(Y.as2, 1)
+    A.wait_ge(Y.vq, 8)
+    A.activation(z1, y1, F.Identity, scale=s2).then_inc(Y.az, 1)
+    A.wait_ge(Y.axc, 1)
+    A.wait_ge(Y.vq, 10)
+    A.activation(T.ys[:, H:], T.xc[:, H:], F.Identity, scale=rs).then_inc(Y.ay, 1)
+
+    V.wait_ge(Y.a2, 1)
+    V.wait_ge(Y.p1, in1)
+    V.wait_ge(Y.p2, in2)
+    V.tensor_reduce(sS, nms, AxisListType.X, OP.add).then_inc(Y.vs, 1)
+    V.wait_ge(Y.at0, 1)
+    V.wait_ge(Y.aq, 1)
+    n = [0]
+
+    def step(ins):
+        n[0] += 1
+        ins.then_inc(Y.vq, 1)
+        V.wait_ge(Y.vq, n[0])
+
+    step(V.tensor_scalar(v, sQ, 1.0 / (N * N * N), t0, OP.mult, OP.add))
+    step(V.tensor_scalar(T.cmp[:], T.tab[:], v, 0.5, OP.is_gt, OP.max))
+    step(V.tensor_reduce(s, T.cmp[:], AxisListType.X, OP.mult))
+    step(V.tensor_scalar(gg, v, s, s, OP.mult, OP.mult))
+    step(V.tensor_scalar(pp, gg, SEED2, SEED1, OP.mult, OP.add))
+    step(V.tensor_scalar(y0, pp, gg, SEED0, OP.mult, OP.add))
+    step(V.tensor_scalar(t1, gg, y0, y0, OP.mult, OP.mult))
+    step(V.tensor_scalar(y1, t1, 1.5, y0, OP.subtract, OP.mult))
+    step(V.tensor_scalar(t2, gg, y1, y1, OP.mult, OP.mult))
+    V.wait_ge(Y.az, 1)
+    step(V.tensor_scalar(rs, t2, 1.5, z1, OP.subtract, OP.mult))
+    V.wait_ge(Y.axc, 1)
+    V.tensor_scalar(T.ys[:, :H], T.xc[:, :H], rs, None, OP.mult).then_inc(Y.vy, 1)
+
+    S.wait_ge(Y.vy, 1)
+    S.wait_ge(Y.ay, 1)
+    S.dma_start(T.y[:], T.ys[:]).then_inc(Y.stq, 16)
+    S.wait_ge(Y.stq, 16)

@@ -1,27 +1,18 @@
-import math
 from concourse.bass import DstId, RemoteDMATransfer
 from concourse.mybir import AluOpType, AxisListType, ActivationFunctionType
 
 N = 6
 TK = 128
 EPS = 0.01
-KT = 64
-ENGINES = 8
-
-SEED2, SEED1, SEED0 = 6707.0017479, -420.44720354, 10.68373326
 
 SCRATCH = {
     "xs": ("sbuf", [128, TK], "float32"),
     "xc": ("sbuf", [128, TK], "float32"),
     "ys": ("sbuf", [128, TK], "float32"),
     "st": ("sbuf", [128, 16], "float32"),
-    "two": ("sbuf", [128, KT], "float32"),
-    "tab": ("sbuf", [128, KT], "float32"),
-    "cmp": ("sbuf", [128, KT], "float32"),
     "sm": ("sbuf", [128, 32], "float32"),
 }
-SEMAPHORES = ["ld", "a1", "a2", "p1", "p2", "snt", "vt", "vs", "at0", "aq", "anm", "axc", "as2", "az", "vq", "vy", "ay",
-              "stq"]
+SEMAPHORES = ["ld", "a1", "a2", "p1", "p2", "snt", "vs", "at0", "aq", "asd", "vn", "vx", "vr", "vy", "ay", "stq"]
 
 
 def _links(topo, a, b):
@@ -74,16 +65,6 @@ def _plan(cores, topo):
     return best[1], best[2]
 
 
-def _engines(mask, most):
-    out, k, e = 0, 0, 0
-    while mask >> e:
-        if (mask >> e) & 1 and k < most:
-            out |= 1 << e
-            k += 1
-        e += 1
-    return out
-
-
 def _count(mask):
     return bin(mask).count("1")
 
@@ -97,14 +78,14 @@ def rank_program(g, core, T, topo):
     partner = [b if a == rank else a for a, b in pairs if rank in (a, b)][0]
 
     def mask1(src, dst):
-        return _engines(topo.mask(cores[src], cores[dst]), ENGINES)
+        return topo.mask(cores[src], cores[dst])
 
     def mask2(src):
         ms = [topo.mask(cores[src], cores[b]) for c, b in hop2 if c == src]
         m = ms[0]
         for o in ms[1:]:
             m &= o
-        return _engines(m, ENGINES)
+        return m
 
     def slot(src, dst):
         k = sorted(c for c, b in hop2 if b == dst).index(src)
@@ -116,16 +97,11 @@ def rank_program(g, core, T, topo):
     S, V, A, Y = g.sync, g.vector, g.scalar, T.sem
     F, OP = ActivationFunctionType, AluOpType
     sm = T.sm
-    t0, sS, sQ, nmu, v, s, gg, pp, y0, t1, y1, t2, rs, s2, z1 = [sm[:, i:i + 1] for i in range(15)]
+    t0, sS, sQ, nmu, sd, rs = [sm[:, i:i + 1] for i in range(6)]
     nms, m2s = T.st[:, 2:14:2], T.st[:, 3:14:2]
     H = TK // 2
 
     S.dma_start(T.xs[:], T.x[:]).then_inc(Y.ld, 16)
-
-    V.memset(T.two[:], 2.0).then_inc(Y.vt, 1)
-    V.wait_ge(Y.vt, 1)
-    V.tensor_tensor_scan(T.tab[:], T.two[:], T.two[:], 2.0 ** -7, OP.mult, OP.mult).then_inc(Y.vt, 1)
-    V.wait_ge(Y.vt, 2)
 
     A.wait_ge(Y.ld, 16)
     A.activation(T.xc[:], T.xs[:], F.Identity, scale=-1.0 / TK, accum_out=T.st[:, 2:3]).then_inc(Y.a1, 1)
@@ -152,43 +128,26 @@ def rank_program(g, core, T, topo):
     A.activation(sm[:, 16:22], m2s, F.Identity, bias=EPS / N, scale=1.0 / (N * TK), accum_out=t0).then_inc(Y.at0, 1)
     A.wait_ge(Y.vs, 1)
     A.activation(sm[:, 24:30], nms, F.Square, bias=sS, scale=-float(N), accum_out=sQ).then_inc(Y.aq, 1)
-    A.activation(nmu, sS, F.Identity, scale=1.0 / N).then_inc(Y.anm, 1)
-    A.wait_ge(Y.anm, 1)
-    A.activation(T.xc[:], T.xs[:], F.Identity, bias=nmu).then_inc(Y.axc, 1)
-    A.wait_ge(Y.vq, 3)
-    A.activation(s2, s, F.Identity, scale=math.sqrt(2.0)).then_inc(Y.as2, 1)
-    A.wait_ge(Y.as2, 1)
-    A.wait_ge(Y.vq, 8)
-    A.activation(z1, y1, F.Identity, scale=s2).then_inc(Y.az, 1)
-    A.wait_ge(Y.axc, 1)
-    A.wait_ge(Y.vq, 10)
+    A.wait_ge(Y.at0, 1)
+    A.wait_ge(Y.aq, 1)
+    A.activation(sd, sQ, F.Sqrt, bias=t0, scale=1.0 / (N * N * N)).then_inc(Y.asd, 1)
+    A.wait_ge(Y.vx, 1)
+    A.wait_ge(Y.vr, 1)
     A.activation(T.ys[:, H:], T.xc[:, H:], F.Identity, scale=rs).then_inc(Y.ay, 1)
 
+    V.wait_ge(Y.ld, 16)
     V.wait_ge(Y.a2, 1)
     V.wait_ge(Y.p1, in1)
     V.wait_ge(Y.p2, in2)
     V.tensor_reduce(sS, nms, AxisListType.X, OP.add).then_inc(Y.vs, 1)
-    V.wait_ge(Y.at0, 1)
-    V.wait_ge(Y.aq, 1)
-    n = [0]
-
-    def step(ins):
-        n[0] += 1
-        ins.then_inc(Y.vq, 1)
-        V.wait_ge(Y.vq, n[0])
-
-    step(V.tensor_scalar(v, sQ, 1.0 / (N * N * N), t0, OP.mult, OP.add))
-    step(V.tensor_scalar(T.cmp[:], T.tab[:], v, 0.5, OP.is_gt, OP.max))
-    step(V.tensor_reduce(s, T.cmp[:], AxisListType.X, OP.mult))
-    step(V.tensor_scalar(gg, v, s, s, OP.mult, OP.mult))
-    step(V.tensor_scalar(pp, gg, SEED2, SEED1, OP.mult, OP.add))
-    step(V.tensor_scalar(y0, pp, gg, SEED0, OP.mult, OP.add))
-    step(V.tensor_scalar(t1, gg, y0, y0, OP.mult, OP.mult))
-    step(V.tensor_scalar(y1, t1, 1.5, y0, OP.subtract, OP.mult))
-    step(V.tensor_scalar(t2, gg, y1, y1, OP.mult, OP.mult))
-    V.wait_ge(Y.az, 1)
-    step(V.tensor_scalar(rs, t2, 1.5, z1, OP.subtract, OP.mult))
-    V.wait_ge(Y.axc, 1)
+    V.wait_ge(Y.vs, 1)
+    V.tensor_scalar(nmu, sS, 1.0 / N, None, OP.mult).then_inc(Y.vn, 1)
+    V.wait_ge(Y.vn, 1)
+    V.tensor_scalar(T.xc[:], T.xs[:], nmu, None, OP.add).then_inc(Y.vx, 1)
+    V.wait_ge(Y.asd, 1)
+    V.reciprocal(rs, sd).then_inc(Y.vr, 1)
+    V.wait_ge(Y.vx, 1)
+    V.wait_ge(Y.vr, 1)
     V.tensor_scalar(T.ys[:, :H], T.xc[:, :H], rs, None, OP.mult).then_inc(Y.vy, 1)
 
     S.wait_ge(Y.vy, 1)

@@ -12,7 +12,7 @@ SCRATCH = {
     "st": ("sbuf", [128, 16], "float32"),
     "sm": ("sbuf", [128, 32], "float32"),
 }
-SEMAPHORES = ["ld", "a1", "a2", "p1", "p2", "snt", "vs", "at0", "aq", "asd", "vn", "vx", "vr", "vy", "ay", "stq"]
+SEMAPHORES = ["ld", "a1", "a2", "p1", "p2", "snt", "vs", "at0", "aq", "asd", "vn", "vv", "vr", "vx", "vy", "ay", "stq"]
 
 
 def _links(topo, a, b):
@@ -97,9 +97,10 @@ def rank_program(g, core, T, topo):
     S, V, A, Y = g.sync, g.vector, g.scalar, T.sem
     F, OP = ActivationFunctionType, AluOpType
     sm = T.sm
-    t0, sS, sQ, nmu, sd, rs = [sm[:, i:i + 1] for i in range(6)]
+    t0, sS, sQ, nmu, sd, vv, iv = [sm[:, i:i + 1] for i in range(7)]
     nms, m2s = T.st[:, 2:14:2], T.st[:, 3:14:2]
     H = TK // 2
+    KQ = 1.0 / (N * N * N)
 
     S.dma_start(T.xs[:], T.x[:]).then_inc(Y.ld, 16)
 
@@ -130,10 +131,10 @@ def rank_program(g, core, T, topo):
     A.activation(sm[:, 24:30], nms, F.Square, bias=sS, scale=-float(N), accum_out=sQ).then_inc(Y.aq, 1)
     A.wait_ge(Y.at0, 1)
     A.wait_ge(Y.aq, 1)
-    A.activation(sd, sQ, F.Sqrt, bias=t0, scale=1.0 / (N * N * N)).then_inc(Y.asd, 1)
+    A.activation(sd, sQ, F.Sqrt, bias=t0, scale=KQ).then_inc(Y.asd, 1)
     A.wait_ge(Y.vx, 1)
-    A.wait_ge(Y.vr, 1)
-    A.activation(T.ys[:, H:], T.xc[:, H:], F.Identity, scale=rs).then_inc(Y.ay, 1)
+    A.wait_ge(Y.asd, 1)
+    A.activation(T.ys[:, H:], T.xc[:, H:], F.Identity, scale=sd).then_inc(Y.ay, 1)
 
     V.wait_ge(Y.ld, 16)
     V.wait_ge(Y.a2, 1)
@@ -142,13 +143,17 @@ def rank_program(g, core, T, topo):
     V.tensor_reduce(sS, nms, AxisListType.X, OP.add).then_inc(Y.vs, 1)
     V.wait_ge(Y.vs, 1)
     V.tensor_scalar(nmu, sS, 1.0 / N, None, OP.mult).then_inc(Y.vn, 1)
+    V.wait_ge(Y.at0, 1)
+    V.wait_ge(Y.aq, 1)
+    V.tensor_scalar(vv, sQ, KQ, t0, OP.mult, OP.add).then_inc(Y.vv, 1)
+    V.wait_ge(Y.vv, 1)
+    V.reciprocal(iv, vv).then_inc(Y.vr, 1)
     V.wait_ge(Y.vn, 1)
-    V.tensor_scalar(T.xc[:], T.xs[:], nmu, None, OP.add).then_inc(Y.vx, 1)
-    V.wait_ge(Y.asd, 1)
-    V.reciprocal(rs, sd).then_inc(Y.vr, 1)
-    V.wait_ge(Y.vx, 1)
     V.wait_ge(Y.vr, 1)
-    V.tensor_scalar(T.ys[:, :H], T.xc[:, :H], rs, None, OP.mult).then_inc(Y.vy, 1)
+    V.tensor_scalar(T.xc[:], T.xs[:], nmu, iv, OP.add, OP.mult).then_inc(Y.vx, 1)
+    V.wait_ge(Y.vx, 1)
+    V.wait_ge(Y.asd, 1)
+    V.tensor_scalar(T.ys[:, :H], T.xc[:, :H], sd, None, OP.mult).then_inc(Y.vy, 1)
 
     S.wait_ge(Y.vy, 1)
     S.wait_ge(Y.ay, 1)

@@ -10,9 +10,10 @@ SCRATCH = {
     "xc": ("sbuf", [128, TK], "float32"),
     "ys": ("sbuf", [128, TK], "float32"),
     "st": ("sbuf", [128, 16], "float32"),
-    "sm": ("sbuf", [128, 32], "float32"),
+    "sm": ("sbuf", [128, 40], "float32"),
 }
-SEMAPHORES = ["ld", "a1", "a2", "p1", "p2", "snt", "vs", "at0", "aq", "asd", "vn", "vv", "vr", "vx", "vy", "ay", "stq"]
+SEMAPHORES = ["ld", "a1", "a2", "p1", "p2", "snt", "ms", "vmo", "as0", "vh", "vk", "au", "ad", "vm", "vn", "vsc", "vr",
+              "asd", "axm", "vy", "stq"]
 
 
 def _links(topo, a, b):
@@ -97,17 +98,25 @@ def rank_program(g, core, T, topo):
     S, V, A, Y = g.sync, g.vector, g.scalar, T.sem
     F, OP = ActivationFunctionType, AluOpType
     sm = T.sm
-    t0, sS, sQ, nmu, sd, vv, iv = [sm[:, i:i + 1] for i in range(7)]
+
+    def col(i):
+        return sm[:, i:i + 1]
+
+    sU, c6, c128, h768 = col(0), col(1), col(2), col(3)
+    c0, sD2, nM2, neh = col(4), col(5), col(6), col(7)
+    vh = col(11)
+    mo, s0, h, nmu, iw, sd = [col(i) for i in range(12, 18)]
+    nm_own, m2_own = T.st[:, 2:3], T.st[:, 3:4]
     nms, m2s = T.st[:, 2:14:2], T.st[:, 3:14:2]
-    H = TK // 2
-    KQ = 1.0 / (N * N * N)
 
     S.dma_start(T.xs[:], T.x[:]).then_inc(Y.ld, 16)
 
     A.wait_ge(Y.ld, 16)
-    A.activation(T.xc[:], T.xs[:], F.Identity, scale=-1.0 / TK, accum_out=T.st[:, 2:3]).then_inc(Y.a1, 1)
+    A.activation(T.xc[:], T.xs[:], F.Identity, scale=-1.0 / TK, accum_out=nm_own).then_inc(Y.a1, 1)
     A.wait_ge(Y.a1, 1)
-    A.activation(T.xc[:], T.xs[:], F.Square, bias=T.st[:, 2:3], accum_out=T.st[:, 3:4]).then_inc(Y.a2, 1)
+    A.activation(T.xc[:], T.xs[:], F.Square, bias=nm_own, accum_out=m2_own).then_inc(Y.a2, 1)
+    A.wait_ge(Y.a2, 1)
+    A.activation(s0, m2_own, F.Sqrt, bias=EPS, scale=1.0 / TK).then_inc(Y.as0, 1)
 
     g.wait_ge(Y.a2, 1)
     rid, pid = topo.addr(cores[partner], core)
@@ -123,39 +132,46 @@ def rank_program(g, core, T, topo):
                        local_sem=Y.snt)
     g.wait_ge(Y.snt, _count(mask1(rank, partner)) + _count(mask2(rank)))
 
-    A.wait_ge(Y.a2, 1)
+    V.memset(c6, 1.0 / N).then_inc(Y.ms, 1)
+    V.memset(c128, -float(TK)).then_inc(Y.ms, 1)
+    V.memset(c0, 0.0).then_inc(Y.ms, 1)
+    V.wait_ge(Y.a1, 1)
+    V.tensor_scalar(mo, nm_own, -1.0, None, OP.mult).then_inc(Y.vmo, 1)
+    V.wait_ge(Y.as0, 1)
+    V.reciprocal(h, s0).then_inc(Y.vh, 1)
+    V.wait_ge(Y.vh, 1)
+    V.tensor_scalar(h768, h, 1.0 / (N * TK), None, OP.mult).then_inc(Y.vk, 1)
+    V.tensor_scalar(neh, h, -EPS, None, OP.mult).then_inc(Y.vk, 1)
+
+    A.wait_ge(Y.vmo, 1)
     A.wait_ge(Y.p1, in1)
     A.wait_ge(Y.p2, in2)
-    A.activation(sm[:, 16:22], m2s, F.Identity, bias=EPS / N, scale=1.0 / (N * TK), accum_out=t0).then_inc(Y.at0, 1)
-    A.wait_ge(Y.vs, 1)
-    A.activation(sm[:, 24:30], nms, F.Square, bias=sS, scale=-float(N), accum_out=sQ).then_inc(Y.aq, 1)
-    A.wait_ge(Y.at0, 1)
-    A.wait_ge(Y.aq, 1)
-    A.activation(sd, sQ, F.Sqrt, bias=t0, scale=KQ).then_inc(Y.asd, 1)
-    A.wait_ge(Y.vx, 1)
-    A.wait_ge(Y.asd, 1)
-    A.activation(T.ys[:, H:], T.xc[:, H:], F.Identity, scale=sd).then_inc(Y.ay, 1)
+    A.activation(sm[:, 20:26], nms, F.Identity, bias=mo, accum_out=sU).then_inc(Y.au, 1)
+    A.activation(sm[:, 28:34], nms, F.Square, bias=mo, accum_out=sD2).then_inc(Y.ad, 1)
+    A.wait_ge(Y.vn, 1)
+    A.activation(T.xc[:], T.xs[:], F.Identity, bias=nmu).then_inc(Y.axm, 1)
+    A.wait_ge(Y.vh, 1)
+    A.wait_ge(Y.vsc, 1)
+    A.activation(sd, vh, F.Sqrt, scale=h).then_inc(Y.asd, 1)
 
-    V.wait_ge(Y.ld, 16)
     V.wait_ge(Y.a2, 1)
     V.wait_ge(Y.p1, in1)
     V.wait_ge(Y.p2, in2)
-    V.tensor_reduce(sS, nms, AxisListType.X, OP.add).then_inc(Y.vs, 1)
-    V.wait_ge(Y.vs, 1)
-    V.tensor_scalar(nmu, sS, 1.0 / N, None, OP.mult).then_inc(Y.vn, 1)
-    V.wait_ge(Y.at0, 1)
-    V.wait_ge(Y.aq, 1)
-    V.tensor_scalar(vv, sQ, KQ, t0, OP.mult, OP.add).then_inc(Y.vv, 1)
-    V.wait_ge(Y.vv, 1)
-    V.reciprocal(iv, vv).then_inc(Y.vr, 1)
-    V.wait_ge(Y.vn, 1)
+    V.tensor_reduce(nM2, m2s, AxisListType.X, OP.add, negate=True).then_inc(Y.vm, 1)
+    V.wait_ge(Y.au, 1)
+    V.tensor_scalar(nmu, sU, 1.0 / N, nm_own, OP.mult, OP.add).then_inc(Y.vn, 1)
+    V.wait_ge(Y.ms, 3)
+    V.wait_ge(Y.vk, 2)
+    V.wait_ge(Y.vm, 1)
+    V.wait_ge(Y.ad, 1)
+    V.tensor_tensor_scan(sm[:, 8:12], sm[:, 0:4], sm[:, 4:8], sU, OP.mult, OP.subtract).then_inc(Y.vsc, 1)
+    V.wait_ge(Y.vsc, 1)
+    V.reciprocal(iw, vh).then_inc(Y.vr, 1)
     V.wait_ge(Y.vr, 1)
-    V.tensor_scalar(T.xc[:], T.xs[:], nmu, iv, OP.add, OP.mult).then_inc(Y.vx, 1)
-    V.wait_ge(Y.vx, 1)
     V.wait_ge(Y.asd, 1)
-    V.tensor_scalar(T.ys[:, :H], T.xc[:, :H], sd, None, OP.mult).then_inc(Y.vy, 1)
+    V.wait_ge(Y.axm, 1)
+    V.tensor_scalar(T.ys[:], T.xc[:], iw, sd, OP.mult, OP.mult).then_inc(Y.vy, 1)
 
     S.wait_ge(Y.vy, 1)
-    S.wait_ge(Y.ay, 1)
     S.dma_start(T.y[:], T.ys[:]).then_inc(Y.stq, 16)
     S.wait_ge(Y.stq, 16)

from concourse.bass import DstId, RemoteDMATransfer
from concourse.mybir import AluOpType, AxisListType, ActivationFunctionType

N = 6
TK = 128
EPS = 0.01

SCRATCH = {
    "xs": ("sbuf", [128, TK], "float32"),
    "xc": ("sbuf", [128, TK], "float32"),
    "ys": ("sbuf", [128, TK], "float32"),
    "st": ("sbuf", [128, 16], "float32"),
    "sm": ("sbuf", [128, 40], "float32"),
}
SEMAPHORES = ["ld", "a1", "a2", "p1", "p2", "snt", "ms", "vmo", "as0", "vh", "vk", "au", "ad", "vm", "vn", "vsc", "vr",
              "asd", "axm", "vy", "stq"]


def _links(topo, a, b):
    if topo.mates(a, b) or topo.same_plane(a, b):
        return 1
    if topo.rack(topo.host(a)) == topo.rack(topo.host(b)):
        return 2
    return 1 if topo.chip(a) == topo.chip(b) else 3


def _matchings(items):
    if not items:
        return [[]]
    a, out = items[0], []
    for b in items[1:]:
        rest = [i for i in items[1:] if i != b]
        out += [[(a, b)] + m for m in _matchings(rest)]
    return out


def _products(opts):
    out = [[]]
    for o in opts:
        out = [p + [c] for p in out for c in o]
    return out


def _plan(cores, topo):
    n = len(cores)

    def ok(a, b):
        return topo.may_write(cores[a], cores[b])

    def ln(a, b):
        return _links(topo, cores[a], cores[b])

    best = None
    for m in _matchings(list(range(n))):
        if not all(ok(a, b) and ok(b, a) for a, b in m):
            continue
        needs = [(b, p) for b in range(n) for p in m if b not in p]
        opts = [[c for c in p if ok(c, b)] for b, p in needs]
        if not all(opts):
            continue
        hop1 = sum(ln(a, b) + ln(b, a) for a, b in m)
        for pick in _products(opts):
            cost = (max(pick.count(c) for c in range(n)), hop1, sum(ln(c, bp[0]) for c, bp in zip(pick, needs)))
            if best is None or cost < best[0]:
                best = (cost, m, [(c, bp[0]) for c, bp in zip(pick, needs)])
    return best[1], best[2]


def _count(mask):
    return bin(mask).count("1")


def rank_program(g, core, T, topo):
    rank = T.rank_of(core)
    if rank is None:
        return
    cores = list(T.cores)
    pairs, hop2 = _plan(cores, topo)
    partner = [b if a == rank else a for a, b in pairs if rank in (a, b)][0]

    def mask1(src, dst):
        return topo.mask(cores[src], cores[dst])

    def mask2(src):
        ms = [topo.mask(cores[src], cores[b]) for c, b in hop2 if c == src]
        m = ms[0]
        for o in ms[1:]:
            m &= o
        return m

    def slot(src, dst):
        k = sorted(c for c, b in hop2 if b == dst).index(src)
        return T.st[:, 6 + 4 * k:10 + 4 * k]

    in1 = _count(mask1(partner, rank))
    in2 = sum(_count(mask2(c)) for c, b in hop2 if b == rank)

    S, V, A, Y = g.sync, g.vector, g.scalar, T.sem
    F, OP = ActivationFunctionType, AluOpType
    sm = T.sm

    def col(i):
        return sm[:, i:i + 1]

    sU, c6, c128, h768 = col(0), col(1), col(2), col(3)
    c0, sD2, nM2, neh = col(4), col(5), col(6), col(7)
    vh = col(11)
    mo, s0, h, nmu, iw, sd = [col(i) for i in range(12, 18)]
    nm_own, m2_own = T.st[:, 2:3], T.st[:, 3:4]
    nms, m2s = T.st[:, 2:14:2], T.st[:, 3:14:2]

    S.dma_start(T.xs[:], T.x[:]).then_inc(Y.ld, 16)

    A.wait_ge(Y.ld, 16)
    A.activation(T.xc[:], T.xs[:], F.Identity, scale=-1.0 / TK, accum_out=nm_own).then_inc(Y.a1, 1)
    A.wait_ge(Y.a1, 1)
    A.activation(T.xc[:], T.xs[:], F.Square, bias=nm_own, accum_out=m2_own).then_inc(Y.a2, 1)
    A.wait_ge(Y.a2, 1)
    A.activation(s0, m2_own, F.Sqrt, bias=EPS, scale=1.0 / TK).then_inc(Y.as0, 1)

    g.wait_ge(Y.a2, 1)
    rid, pid = topo.addr(cores[partner], core)
    g.remote_dma(T.st[:, 4:6], T.st[:, 2:4], Y.p1, Y.snt, pid, rid, mask1(rank, partner))
    g.wait_ge(Y.p1, in1)
    outs = [b for c, b in hop2 if c == rank]
    ids = []
    for b in outs:
        rid, pid = topo.addr(cores[b], core)
        ids.append(DstId(rid=rid, pnc=pid))
    g.remote_dma_fused([RemoteDMATransfer(dst_ids=ids, dma_engine_mask=mask2(rank), remote_sem=Y.p2,
                                          srcs=[T.st[:, 2:6]], dsts=[slot(rank, b) for b in outs], alu_op=0)],
                       local_sem=Y.snt)
    g.wait_ge(Y.snt, _count(mask1(rank, partner)) + _count(mask2(rank)))

    V.memset(c6, 1.0 / N).then_inc(Y.ms, 1)
    V.memset(c128, -float(TK)).then_inc(Y.ms, 1)
    V.memset(c0, 0.0).then_inc(Y.ms, 1)
    V.wait_ge(Y.a1, 1)
    V.tensor_scalar(mo, nm_own, -1.0, None, OP.mult).then_inc(Y.vmo, 1)
    V.wait_ge(Y.as0, 1)
    V.reciprocal(h, s0).then_inc(Y.vh, 1)
    V.wait_ge(Y.vh, 1)
    V.tensor_scalar(h768, h, 1.0 / (N * TK), None, OP.mult).then_inc(Y.vk, 1)
    V.tensor_scalar(neh, h, -EPS, None, OP.mult).then_inc(Y.vk, 1)

    A.wait_ge(Y.vmo, 1)
    A.wait_ge(Y.p1, in1)
    A.wait_ge(Y.p2, in2)
    A.activation(sm[:, 20:26], nms, F.Identity, bias=mo, accum_out=sU).then_inc(Y.au, 1)
    A.activation(sm[:, 28:34], nms, F.Square, bias=mo, accum_out=sD2).then_inc(Y.ad, 1)
    A.wait_ge(Y.vn, 1)
    A.activation(T.xc[:], T.xs[:], F.Identity, bias=nmu).then_inc(Y.axm, 1)
    A.wait_ge(Y.vh, 1)
    A.wait_ge(Y.vsc, 1)
    A.activation(sd, vh, F.Sqrt, scale=h).then_inc(Y.asd, 1)

    V.wait_ge(Y.a2, 1)
    V.wait_ge(Y.p1, in1)
    V.wait_ge(Y.p2, in2)
    V.tensor_reduce(nM2, m2s, AxisListType.X, OP.add, negate=True).then_inc(Y.vm, 1)
    V.wait_ge(Y.au, 1)
    V.tensor_scalar(nmu, sU, 1.0 / N, nm_own, OP.mult, OP.add).then_inc(Y.vn, 1)
    V.wait_ge(Y.ms, 3)
    V.wait_ge(Y.vk, 2)
    V.wait_ge(Y.vm, 1)
    V.wait_ge(Y.ad, 1)
    V.tensor_tensor_scan(sm[:, 8:12], sm[:, 0:4], sm[:, 4:8], sU, OP.mult, OP.subtract).then_inc(Y.vsc, 1)
    V.wait_ge(Y.vsc, 1)
    V.reciprocal(iw, vh).then_inc(Y.vr, 1)
    V.wait_ge(Y.vr, 1)
    V.wait_ge(Y.asd, 1)
    V.wait_ge(Y.axm, 1)
    V.tensor_scalar(T.ys[:], T.xc[:], iw, sd, OP.mult, OP.mult).then_inc(Y.vy, 1)

    S.wait_ge(Y.vy, 1)
    S.dma_start(T.y[:], T.ys[:]).then_inc(Y.stq, 16)
    S.wait_ge(Y.stq, 16)
